import numpy as np
import ml_dtypes


def mxq(x, axis, fmt="e4m3"):
    dtype, down = {"e4m3": (ml_dtypes.float8_e4m3fn, 7), "e5m2": (ml_dtypes.float8_e5m2, 14)}[fmt]
    v = np.moveaxis(np.asarray(x, np.float32).astype(ml_dtypes.bfloat16).astype(np.float64), axis, -1)
    blocks = v.reshape(v.shape[:-1] + (-1, 32))
    amax = np.abs(blocks).max(-1, keepdims=True)
    byte = np.maximum(np.where(amax > 0, np.frexp(amax)[1] - 1 + 127, 0) - down, 1)
    scale = np.exp2(byte - 127.0)
    codes = (blocks / scale).astype(np.float32).astype(dtype).astype(np.float64)
    return np.moveaxis((codes * scale).reshape(v.shape), -1, axis)


WIDE = False


def mx_kscale(k):
    if not WIDE:
        return np.ones(k)
    levels = np.array([10, -10, 5, -5, 0])
    if k % 512:
        return np.exp2(np.random.permutation(np.resize(levels, k // 32))).repeat(32)
    a = np.empty((k // 512, 16))
    for p in range(k // 512):
        a[p, :8] = np.random.permutation(np.resize(levels, 8))
        for g in range(8):
            far = levels[np.abs(levels - a[p, g]) >= 10]
            a[p, g + 8] = far[np.random.randint(len(far))]
    return np.exp2(a.ravel()).repeat(32)


def f64(x):
    return np.asarray(x).astype(np.float64)


def striped(idx):
    return np.tile(np.asarray(idx).reshape(-1, 16).T, (8, 1)).astype(np.uint16)


def unstriped(offs):
    return offs[:16].T.reshape(-1).astype(np.int64)


def striped8(idx):
    return np.asarray(idx).reshape(8, -1, 16).transpose(0, 2, 1).reshape(128, -1).astype(np.uint16)


def unstriped8(offs):
    return offs.reshape(8, 16, -1).transpose(0, 2, 1).reshape(8, -1).astype(np.int64)


def pick8(x, idx, run):
    r = np.arange(len(x))
    return x[r[:, None], idx[r % (8 * run) // run]]


E2M1 = np.array([0.0, 0.5, 1.0, 1.5, 2.0, 3.0, 4.0, 6.0, -0.0, -0.5, -1.0, -1.5, -2.0, -3.0, -4.0, -6.0])


def pack_weight(w, fmt):
    k, n = w.shape
    w = f64(np.asarray(w, np.float32).astype(ml_dtypes.bfloat16)).reshape(k // 32, 32, n)
    amax = np.abs(w).max(1)
    if fmt == "e4m3":
        byte = np.frexp(amax)[1] - 1 + 127 - 7
    else:
        mant, ex = np.frexp(amax / 6.0)
        byte = np.where(mant > 0.5, ex, ex - 1) + 127
    byte = np.clip(np.where(amax > 0, byte, 1), 1, 254)
    scaled = (w * np.exp2(127.0 - byte)[:, None, :]).reshape(k, n).astype(np.float32)
    by_word = np.ascontiguousarray(scaled.reshape(k // 512, 128, 4, n).transpose(0, 1, 3, 2))
    if fmt == "e4m3":
        words = by_word.astype(ml_dtypes.float8_e4m3fn).view(np.uint8)
    else:
        c = by_word.astype(ml_dtypes.float4_e2m1fn).view(np.uint8) & 0xF
        words = (c[..., 0::2] | (c[..., 1::2] << 4)).reshape(k // 512, 128, 2 * n)
    return np.ascontiguousarray(words), np.ascontiguousarray(byte.astype(np.uint8).reshape(k // 512, 16, n))


def unpack_weight(words, scales, fmt):
    g, _, n = scales.shape
    words = np.ascontiguousarray(words).reshape(g, 128, n, -1)
    if fmt == "e4m3":
        vals = words.view(ml_dtypes.float8_e4m3fn).astype(np.float64)
    else:
        nib = np.empty((g, 128, n, 4), np.uint8)
        nib[..., 0::2] = words & 0xF
        nib[..., 1::2] = words >> 4
        vals = E2M1[nib]
    vals = vals * np.repeat(np.exp2(scales.astype(np.float64) - 127.0), 8, axis=1)[..., None]
    return vals.transpose(0, 1, 3, 2).reshape(g * 512, n)


def sigmoid(v):
    return 1.0 / (1.0 + np.exp(-v))


K, R, F, T, J, U, M = 512, 128, 512, 2048, 512, 1024, 256


def setup_inputs():
    n = np.random.standard_normal
    idx = np.random.permutation(T)[:J]
    idx2 = np.stack([np.random.permutation(U)[:J] for _ in range(8)])
    idx3 = np.stack([np.random.permutation(U)[:M] for _ in range(8)])
    fk = mx_kscale(K)
    ff = mx_kscale(F)
    tabp = pack_weight(n((K, T)) / fk[:, None], "e4m3")
    return {
        "tab_words": tabp[0],
        "tab_scales": tabp[1],
        "w1": (n((K, R)) * 1 / np.sqrt(K) * fk[:, None]).astype(np.float32),
        "gain": (np.random.uniform(0.5, 1.5, (R, 1))).astype(np.float32),
        "pb": (np.random.uniform(0.3, 1.0, (1, M))).astype(np.float32),
        "wo": (n((F, R)) * 1 / np.sqrt(F) * ff[:, None]).astype(np.float32),
        "dy": (n((F, M)) / ff[:, None]).astype(np.float32),
        "og": (np.random.uniform(0.3, 1.0, (R, 1))).astype(np.float32),
        "base": (0.3 * n((R, J))).astype(np.float32),
        "offs": striped(idx),
        "offs2": striped8(idx2),
        "offs3": striped8(idx3),
    }


def reference(tab_words, tab_scales, w1, gain, pb, wo, dy, og, base, offs, offs2, offs3):
    idx = unstriped(offs)
    idx2 = unstriped8(offs2)
    idx3 = unstriped8(offs3)
    tabu = unpack_weight(tab_words, tab_scales, "e4m3")
    w1q = mxq(f64(w1), 0, "e4m3")
    tabidxg = tabu[:, idx]
    a = w1q.T @ tabidxg
    h1 = np.tanh(a)
    h2 = h1 * f64(gain)
    pg = np.zeros((R, U))
    pg[np.arange(R)[:, None], idx2[np.arange(R) % 128 // 16]] = h2
    s = pick8(pg, idx3, 16) + f64(pb)
    woq = mxq(f64(wo), 0, "e4m3")
    dyq = mxq(f64(dy), 0, "e4m3")
    c0 = woq.T @ dyq
    ds = c0 * sigmoid(s) + c0 * s * sigmoid(s) * (1.0 - sigmoid(s))
    s1 = np.zeros((R, U))
    s1[np.arange(R)[:, None], idx3[np.arange(R) % 128 // 16]] = ds
    dh2 = pick8(s1, idx2, 16)
    dh1 = dh2 * f64(gain)
    da = dh1 * (1.0 - np.square(h1))
    hda = da * 2.0
    hdh1 = hda * (1.0 - np.square(h1))
    hdh2 = hdh1 * f64(gain)
    s51 = np.zeros((R, U))
    s51[np.arange(R)[:, None], idx2[np.arange(R) % 128 // 16]] = hdh2
    hds = pick8(s51, idx3, 16)
    hs = hds * c0 * sigmoid(s) * (1.0 - sigmoid(s)) + hds * (1.0 - sigmoid(s)) * sigmoid(s) * c0 + hds * (1.0 - sigmoid(s)) * c0 * s * sigmoid(s) * (1.0 - sigmoid(s)) + hds * c0 * s * sigmoid(s) * (-1.0) * sigmoid(s) * (1.0 - sigmoid(s))
    s52 = np.zeros((R, U))
    s52[np.arange(R)[:, None], idx3[np.arange(R) % 128 // 16]] = hs
    hh2 = pick8(s52, idx2, 16)
    hh1 = hda * dh1 * (-1.0) * h1 * 2.0 + hh2 * f64(gain)
    ha = hh1 * (1.0 - np.square(h1))
    y = ha * f64(og) + f64(base)
    return y

@@ -1,0 +1,195 @@
+from contextlib import ExitStack
+
+import concourse.mybir as mybir
+from concourse.masks import make_identity
+
+K, R, F, T, J, U, M = 512, 128, 512, 2048, 512, 1024, 256
+FLOPS = 2 * K * R * J + 2 * F * R * M
+
+F32 = mybir.dt.float32
+BF16 = mybir.dt.bfloat16
+I32 = mybir.dt.int32
+U32 = mybir.dt.uint32
+U16 = mybir.dt.uint16
+U8 = mybir.dt.uint8
+FP8X4 = mybir.dt.float8_e4m3fn_x4
+ACT = mybir.ActivationFunctionType
+ALU = mybir.AluOpType
+
+P = 128
+PACK = 4
+HALF = J // 2
+COLS = 16
+LEAD = 512
+
+
+def interleaved_views(grouped, raw):
+    dst = grouped[:].rearrange("p (c i) t -> p c t i", i=4)
+    src = raw[:].rearrange("p t (c i) -> p c t i", i=4)
+    return dst, src
+
+
+def tile_attend_gpwriteread_kernel(tc, tab_words, tab_scales, w1, gain, pb, wo, dy, og, base, offs, offs2, offs3, out):
+    nc = tc.nc
+    with ExitStack() as ctx:
+        sb = ctx.enter_context(tc.tile_pool(name="sb", bufs=1))
+        ps = ctx.enter_context(tc.psum_pool(name="ps", bufs=1))
+
+        def f32(name, width):
+            return sb.tile([P, width], F32, name=name, align_bytes=64)
+
+        halves = [slice(h * HALF, (h + 1) * HALF) for h in range(2)]
+        list_halves = [slice(h * HALF // COLS, (h + 1) * HALF // COLS) for h in range(2)]
+
+        idx = sb.tile([P, J // COLS], U16, name="idx")
+        idx2 = sb.tile([P, J // COLS], U16, name="idx2")
+        idx3 = sb.tile([P, M // COLS], U16, name="idx3")
+        words = sb.tile([P, T], U32, name="words", align_bytes=64)
+        scales = sb.tile([P, T], U8, name="scales", align_bytes=64)
+        w1_raw = sb.tile([P, PACK, R], F32, name="w1_raw")
+        wo_raw = sb.tile([P, PACK, R], F32, name="wo_raw")
+        dy_raw = sb.tile([P, PACK, M], F32, name="dy_raw")
+        base_sb = f32("base_sb", J)
+        g = sb.tile([P, 1], F32, name="g")
+        og_sb = sb.tile([P, 1], F32, name="og_sb")
+        pb_cols = sb.tile([P, 2], F32, name="pb_cols")
+
+        nc.vector.memset(scales[:].bitcast(I32), 0)
+        words_hbm = tab_words[0].rearrange("p c t -> p (c t)").bitcast(I32)
+        nc.sync.dma_start(idx[:], offs)
+        nc.sync.dma_start(words[:, :LEAD].bitcast(I32), words_hbm[:, :LEAD])
+        for quad in range(4):
+            nc.sync.dma_start(
+                scales[32 * quad : 32 * quad + 4, :].bitcast(I32),
+                tab_scales[0, 4 * quad : 4 * quad + 4, :].bitcast(I32),
+            )
+        nc.sync.dma_start(w1_raw[:], w1.rearrange("(p t) r -> p t r", t=PACK))
+        nc.sync.dma_start(words[:, LEAD:].bitcast(I32), words_hbm[:, LEAD:])
+        nc.sync.dma_start(idx2[:], offs2)
+        nc.sync.dma_start(wo_raw[:], wo.rearrange("(p t) r -> p t r", t=PACK))
+        nc.sync.dma_start(dy_raw[:], dy.rearrange("(p t) m -> p t m", t=PACK))
+        nc.sync.dma_start(idx3[:], offs3)
+        nc.sync.dma_start(base_sb[:], base)
+        nc.gpsimd.dma_start(g[:], gain)
+        nc.gpsimd.dma_start(pb_cols[:], pb.rearrange("o (p c) -> p (o c)", c=2))
+        ident = f32("ident", P)
+        make_identity(nc, ident[:])
+        nc.gpsimd.dma_start(og_sb[:], og)
+
+        page_j = f32("page_j", U)
+        page_m = f32("page_m", U)
+        nc.vector.memset(page_j[:], 0.0)
+        nc.vector.memset(page_m[:], 0.0)
+
+
+        w1_bf = sb.tile([P, R, PACK], BF16, name="w1_bf", align_bytes=64)
+        dst, src = interleaved_views(w1_bf, w1_raw)
+        nc.vector.tensor_copy(dst, src)
+        scales_g = sb.tile([P, J], U8, name="scales_g", align_bytes=64)
+        nc.vector.tensor_copy(scales_g[:], scales[:].indirect(idx[:]))
+        w1_q = sb.tile([P, R], U32, name="w1_q", align_bytes=64)
+        w1_s = sb.tile([P, R], U8, name="w1_s", align_bytes=64)
+        nc.vector.quantize_mx(out=w1_q[:].bitcast(FP8X4), scales=w1_s[:], in_=w1_bf[:].rearrange("p r t -> p (r t)"))
+
+        g_wide = f32("g_wide", HALF)
+        nc.scalar.activation(g_wide[:], g[:, 0:1].to_broadcast([P, HALF]), ACT.Copy)
+        neg_g = sb.tile([P, 1], F32, name="neg_g")
+        nc.vector.tensor_scalar(neg_g[:], g[:], -1.0, None, ALU.mult)
+
+        h1 = []
+        for h in range(2):
+            words_g = sb.tile([P, HALF], U32, name="words_g%d" % h, tag="stage%d" % h, align_bytes=64)
+            nc.vector.tensor_copy(words_g[:], words[:].indirect(idx[:, list_halves[h]]))
+            a_ps = ps.tile([P, HALF], F32, name="a_ps%d" % h, tag="bank%d" % h)
+            nc.tensor.matmul_mx(
+                out=a_ps[:], lhsT=w1_q[:].bitcast(FP8X4), lhsT_scale=w1_s[:],
+                rhs=words_g[:].bitcast(FP8X4), rhs_scale=scales_g[:, halves[h]], start=True, stop=True,
+            )
+            t_h = f32("h1_%d" % h, HALF)
+            nc.scalar.activation(t_h[:], a_ps[:], ACT.Tanh)
+            h1.append(t_h)
+
+        wo_bf = sb.tile([P, R, PACK], BF16, name="wo_bf", tag="stage0", align_bytes=64)
+        dst, src = interleaved_views(wo_bf, wo_raw)
+        nc.scalar.copy(dst, src)
+        dy_bf = sb.tile([P, M, PACK], BF16, name="dy_bf", tag="stage1", align_bytes=64)
+        dst, src = interleaved_views(dy_bf, dy_raw)
+        nc.scalar.copy(dst, src)
+
+        pb_ps = ps.tile([P, 2, P], F32, name="pb_ps", tag="bank1")
+        for c in range(2):
+            nc.tensor.transpose(pb_ps[:, c, :], pb_cols[:, c : c + 1].to_broadcast([P, P]), ident[:])
+        pb_wide = f32("pb_wide", M)
+        nc.scalar.copy(pb_wide[:].rearrange("p (n c) -> p n c", c=2), pb_ps[:].rearrange("p c n -> p n c"))
+
+        nc.vector.tensor_tensor(page_j[:].indirect(idx2[:, list_halves[0]]), h1[0][:], g_wide[:], ALU.mult)
+        wo_q = sb.tile([P, R], U32, name="wo_q", align_bytes=64)
+        wo_s = sb.tile([P, R], U8, name="wo_s", align_bytes=64)
+        nc.vector.quantize_mx(out=wo_q[:].bitcast(FP8X4), scales=wo_s[:], in_=wo_bf[:].rearrange("p r t -> p (r t)"))
+        nc.vector.tensor_tensor(page_j[:].indirect(idx2[:, list_halves[1]]), h1[1][:], g_wide[:], ALU.mult)
+        dy_q = sb.tile([P, M], U32, name="dy_q", align_bytes=64)
+        dy_s = sb.tile([P, M], U8, name="dy_s", align_bytes=64)
+        nc.vector.quantize_mx(out=dy_q[:].bitcast(FP8X4), scales=dy_s[:], in_=dy_bf[:].rearrange("p m t -> p (m t)"))
+        c0_ps = ps.tile([P, M], F32, name="c0_ps")
+        nc.tensor.matmul_mx(
+            out=c0_ps[:], lhsT=wo_q[:].bitcast(FP8X4), lhsT_scale=wo_s[:],
+            rhs=dy_q[:].bitcast(FP8X4), rhs_scale=dy_s[:], start=True, stop=True,
+        )
+        c0_half = f32("c0_half", M)
+        nc.scalar.activation(c0_half[:], c0_ps[:], ACT.Copy, scale=0.5)
+
+        s = sb.tile([P, M], F32, name="s", tag="stage1", align_bytes=64)
+        nc.vector.tensor_tensor(s[:], page_j[:].indirect(idx3[:]), pb_wide[:], ALU.add)
+        u = f32("u", M)
+        nc.scalar.activation(u[:], s[:], ACT.Tanh, scale=0.5)
+        uu = f32("uu", M)
+        nc.scalar.activation(uu[:], u[:], ACT.Square)
+        ncs = f32("ncs", M)
+        nc.vector.scalar_tensor_tensor(ncs[:], s[:], -0.5, c0_half[:], ALU.mult, ALU.mult)
+        ds_a = f32("ds_a", M)
+        nc.vector.scalar_tensor_tensor(ds_a[:], u[:], 1.0, c0_half[:], ALU.add, ALU.mult)
+        ds_b = f32("ds_b", M)
+        nc.vector.scalar_tensor_tensor(ds_b[:], uu[:], -1.0, ncs[:], ALU.add, ALU.mult)
+
+        sq = f32("sq", J)
+        for h in range(2):
+            nc.scalar.activation(sq[:, halves[h]], h1[h][:], ACT.Square)
+        gq = f32("gq", J)
+        nc.scalar.activation(gq[:], sq[:], ACT.Identity, bias=g[:], scale=neg_g[:])
+        gq2 = f32("gq2", J)
+        nc.scalar.activation(gq2[:], gq[:], ACT.Copy, scale=2.0)
+        gq_og = f32("gq_og", J)
+        nc.scalar.activation(gq_og[:], gq[:], ACT.Copy, scale=og_sb[:])
+
+        su = f32("su", M)
+        nc.vector.scalar_tensor_tensor(su[:], s[:], 0.5, u[:], ALU.mult, ALU.mult)
+        nc.vector.tensor_tensor(page_m[:].indirect(idx3[:]), ds_a[:], ds_b[:], ALU.add)
+        hs_a = f32("hs_a", M)
+        nc.vector.scalar_tensor_tensor(hs_a[:], uu[:], -1.0, c0_half[:], ALU.add, ALU.mult)
+        hs_b = f32("hs_b", M)
+        nc.scalar.activation(hs_b[:], su[:], ACT.Copy, bias=-1.0)
+
+        da = f32("da", J)
+        nc.vector.tensor_tensor(da[:], page_m[:].indirect(idx2[:]), gq[:], ALU.mult)
+        nc.vector.tensor_tensor(page_j[:].indirect(idx2[:]), da[:], gq2[:], ALU.mult)
+        da_sq = f32("da_sq", J)
+        nc.scalar.activation(da_sq[:], da[:], ACT.Square, scale=2.0)
+        direct = [f32("direct%d" % h, HALF) for h in range(2)]
+        rest = [f32("rest%d" % h, HALF) for h in range(2)]
+
+        nc.vector.scalar_tensor_tensor(direct[0][:], da_sq[:, halves[0]], og_sb[:], h1[0][:], ALU.mult, ALU.mult)
+        hds_a = f32("hds_a", M)
+        nc.vector.tensor_tensor(hds_a[:], page_j[:].indirect(idx3[:]), hs_a[:], ALU.mult)
+        nc.vector.scalar_tensor_tensor(direct[1][:], da_sq[:, halves[1]], og_sb[:], h1[1][:], ALU.mult, ALU.mult)
+        nc.vector.tensor_tensor(page_m[:].indirect(idx3[:]), hds_a[:], hs_b[:], ALU.mult)
+        nc.vector.tensor_tensor(rest[0][:], base_sb[:, halves[0]], direct[0][:], ALU.subtract)
+
+        through = [f32("through%d" % h, HALF) for h in range(2)]
+        res = [f32("res%d" % h, HALF) for h in range(2)]
+        nc.vector.tensor_tensor(through[0][:], page_m[:].indirect(idx2[:, list_halves[0]]), gq_og[:, halves[0]], ALU.mult)
+        nc.vector.tensor_tensor(rest[1][:], base_sb[:, halves[1]], direct[1][:], ALU.subtract)
+        nc.vector.tensor_tensor(res[0][:], through[0][:], rest[0][:], ALU.add)
+        nc.sync.dma_start(out[:, halves[0]], res[0][:])
+        nc.vector.tensor_tensor(through[1][:], page_m[:].indirect(idx2[:, list_halves[1]]), gq_og[:, halves[1]], ALU.mult)
+        nc.vector.tensor_tensor(res[1][:], through[1][:], rest[1][:], ALU.add)
+        nc.scalar.dma_start(out[:, halves[1]], res[1][:])

@@ -20,7 +20,7 @@ P = 128
 PACK = 4
 HALF = J // 2
 COLS = 16
-LEAD = 512
+LEAD = 768
 
 
 def interleaved_views(grouped, raw):
@@ -35,8 +35,8 @@ def tile_attend_gpwriteread_kernel(tc, tab_words, tab_scales, w1, gain, pb, wo, 
         sb = ctx.enter_context(tc.tile_pool(name="sb", bufs=1))
         ps = ctx.enter_context(tc.psum_pool(name="ps", bufs=1))
 
-        def f32(name, width):
-            return sb.tile([P, width], F32, name=name, align_bytes=64)
+        def f32(name, width, tag=None):
+            return sb.tile([P, width], F32, name=name, tag=tag or name, align_bytes=64)
 
         halves = [slice(h * HALF, (h + 1) * HALF) for h in range(2)]
         list_halves = [slice(h * HALF // COLS, (h + 1) * HALF // COLS) for h in range(2)]
@@ -48,55 +48,54 @@ def tile_attend_gpwriteread_kernel(tc, tab_words, tab_scales, w1, gain, pb, wo, 
         scales = sb.tile([P, T], U8, name="scales", align_bytes=64)
         w1_raw = sb.tile([P, PACK, R], F32, name="w1_raw")
         wo_raw = sb.tile([P, PACK, R], F32, name="wo_raw")
-        dy_raw = sb.tile([P, PACK, M], F32, name="dy_raw")
+        dy_raw = sb.tile([P, PACK, M], F32, name="dy_raw", tag="dy_then_pb", align_bytes=64)
         base_sb = f32("base_sb", J)
         g = sb.tile([P, 1], F32, name="g")
         og_sb = sb.tile([P, 1], F32, name="og_sb")
         pb_cols = sb.tile([P, 2], F32, name="pb_cols")
 
-        nc.vector.memset(scales[:].bitcast(I32), 0)
+        nc.gpsimd.memset(scales[:].bitcast(I32), 0)
         words_hbm = tab_words[0].rearrange("p c t -> p (c t)").bitcast(I32)
         nc.sync.dma_start(idx[:], offs)
+        nc.sync.dma_start(w1_raw[:], w1.rearrange("(p t) r -> p t r", t=PACK))
         nc.sync.dma_start(words[:, :LEAD].bitcast(I32), words_hbm[:, :LEAD])
         for quad in range(4):
             nc.sync.dma_start(
                 scales[32 * quad : 32 * quad + 4, :].bitcast(I32),
                 tab_scales[0, 4 * quad : 4 * quad + 4, :].bitcast(I32),
             )
-        nc.sync.dma_start(w1_raw[:], w1.rearrange("(p t) r -> p t r", t=PACK))
         nc.sync.dma_start(words[:, LEAD:].bitcast(I32), words_hbm[:, LEAD:])
+        nc.sync.dma_start(g[:], gain)
         nc.sync.dma_start(idx2[:], offs2)
         nc.sync.dma_start(wo_raw[:], wo.rearrange("(p t) r -> p t r", t=PACK))
         nc.sync.dma_start(dy_raw[:], dy.rearrange("(p t) m -> p t m", t=PACK))
+        nc.sync.dma_start(pb_cols[:], pb.rearrange("o (p c) -> p (o c)", c=2))
         nc.sync.dma_start(idx3[:], offs3)
+        nc.sync.dma_start(og_sb[:], og)
         nc.sync.dma_start(base_sb[:], base)
-        nc.gpsimd.dma_start(g[:], gain)
-        nc.gpsimd.dma_start(pb_cols[:], pb.rearrange("o (p c) -> p (o c)", c=2))
+
         ident = f32("ident", P)
         make_identity(nc, ident[:])
-        nc.gpsimd.dma_start(og_sb[:], og)
-
         page_j = f32("page_j", U)
         page_m = f32("page_m", U)
         nc.vector.memset(page_j[:], 0.0)
         nc.vector.memset(page_m[:], 0.0)
 
-
         w1_bf = sb.tile([P, R, PACK], BF16, name="w1_bf", align_bytes=64)
         dst, src = interleaved_views(w1_bf, w1_raw)
         nc.vector.tensor_copy(dst, src)
-        scales_g = sb.tile([P, J], U8, name="scales_g", align_bytes=64)
-        nc.vector.tensor_copy(scales_g[:], scales[:].indirect(idx[:]))
         w1_q = sb.tile([P, R], U32, name="w1_q", align_bytes=64)
         w1_s = sb.tile([P, R], U8, name="w1_s", align_bytes=64)
         nc.vector.quantize_mx(out=w1_q[:].bitcast(FP8X4), scales=w1_s[:], in_=w1_bf[:].rearrange("p r t -> p (r t)"))
+        scales_g = sb.tile([P, J], U8, name="scales_g", align_bytes=64)
+        nc.vector.tensor_copy(scales_g[:], scales[:].indirect(idx[:]))
 
         g_wide = f32("g_wide", HALF)
         nc.scalar.activation(g_wide[:], g[:, 0:1].to_broadcast([P, HALF]), ACT.Copy)
         neg_g = sb.tile([P, 1], F32, name="neg_g")
-        nc.vector.tensor_scalar(neg_g[:], g[:], -1.0, None, ALU.mult)
+        nc.scalar.activation(neg_g[:], g[:], ACT.Copy, scale=-1.0)
 
-        h1 = []
+        h1 = f32("h1", J)
         for h in range(2):
             words_g = sb.tile([P, HALF], U32, name="words_g%d" % h, tag="stage%d" % h, align_bytes=64)
             nc.vector.tensor_copy(words_g[:], words[:].indirect(idx[:, list_halves[h]]))
@@ -105,9 +104,7 @@ def tile_attend_gpwriteread_kernel(tc, tab_words, tab_scales, w1, gain, pb, wo, 
                 out=a_ps[:], lhsT=w1_q[:].bitcast(FP8X4), lhsT_scale=w1_s[:],
                 rhs=words_g[:].bitcast(FP8X4), rhs_scale=scales_g[:, halves[h]], start=True, stop=True,
             )
-            t_h = f32("h1_%d" % h, HALF)
-            nc.scalar.activation(t_h[:], a_ps[:], ACT.Tanh)
-            h1.append(t_h)
+            nc.scalar.activation(h1[:, halves[h]], a_ps[:], ACT.Tanh)
 
         wo_bf = sb.tile([P, R, PACK], BF16, name="wo_bf", tag="stage0", align_bytes=64)
         dst, src = interleaved_views(wo_bf, wo_raw)
@@ -119,14 +116,14 @@ def tile_attend_gpwriteread_kernel(tc, tab_words, tab_scales, w1, gain, pb, wo, 
         pb_ps = ps.tile([P, 2, P], F32, name="pb_ps", tag="bank1")
         for c in range(2):
             nc.tensor.transpose(pb_ps[:, c, :], pb_cols[:, c : c + 1].to_broadcast([P, P]), ident[:])
-        pb_wide = f32("pb_wide", M)
+        pb_wide = f32("pb_wide", M, tag="dy_then_pb")
         nc.scalar.copy(pb_wide[:].rearrange("p (n c) -> p n c", c=2), pb_ps[:].rearrange("p c n -> p n c"))
 
-        nc.vector.tensor_tensor(page_j[:].indirect(idx2[:, list_halves[0]]), h1[0][:], g_wide[:], ALU.mult)
+        nc.vector.tensor_tensor(page_j[:].indirect(idx2[:, list_halves[0]]), h1[:, halves[0]], g_wide[:], ALU.mult)
         wo_q = sb.tile([P, R], U32, name="wo_q", align_bytes=64)
         wo_s = sb.tile([P, R], U8, name="wo_s", align_bytes=64)
         nc.vector.quantize_mx(out=wo_q[:].bitcast(FP8X4), scales=wo_s[:], in_=wo_bf[:].rearrange("p r t -> p (r t)"))
-        nc.vector.tensor_tensor(page_j[:].indirect(idx2[:, list_halves[1]]), h1[1][:], g_wide[:], ALU.mult)
+        nc.vector.tensor_tensor(page_j[:].indirect(idx2[:, list_halves[1]]), h1[:, halves[1]], g_wide[:], ALU.mult)
         dy_q = sb.tile([P, M], U32, name="dy_q", align_bytes=64)
         dy_s = sb.tile([P, M], U8, name="dy_s", align_bytes=64)
         nc.vector.quantize_mx(out=dy_q[:].bitcast(FP8X4), scales=dy_s[:], in_=dy_bf[:].rearrange("p m t -> p (m t)"))
@@ -135,61 +132,65 @@ def tile_attend_gpwriteread_kernel(tc, tab_words, tab_scales, w1, gain, pb, wo, 
             out=c0_ps[:], lhsT=wo_q[:].bitcast(FP8X4), lhsT_scale=wo_s[:],
             rhs=dy_q[:].bitcast(FP8X4), rhs_scale=dy_s[:], start=True, stop=True,
         )
-        c0_half = f32("c0_half", M)
-        nc.scalar.activation(c0_half[:], c0_ps[:], ACT.Copy, scale=0.5)
 
-        s = sb.tile([P, M], F32, name="s", tag="stage1", align_bytes=64)
+        s = f32("s", M)
         nc.vector.tensor_tensor(s[:], page_j[:].indirect(idx3[:]), pb_wide[:], ALU.add)
         u = f32("u", M)
         nc.scalar.activation(u[:], s[:], ACT.Tanh, scale=0.5)
-        uu = f32("uu", M)
-        nc.scalar.activation(uu[:], u[:], ACT.Square)
-        ncs = f32("ncs", M)
-        nc.vector.scalar_tensor_tensor(ncs[:], s[:], -0.5, c0_half[:], ALU.mult, ALU.mult)
-        ds_a = f32("ds_a", M)
-        nc.vector.scalar_tensor_tensor(ds_a[:], u[:], 1.0, c0_half[:], ALU.add, ALU.mult)
-        ds_b = f32("ds_b", M)
-        nc.vector.scalar_tensor_tensor(ds_b[:], uu[:], -1.0, ncs[:], ALU.add, ALU.mult)
+        v = f32("v", M, tag="v_then_gq_og")
+        nc.vector.scalar_tensor_tensor(v[:], u[:], -1.0, s[:], ALU.add, ALU.mult)
+        x = f32("x", M)
+        nc.vector.scalar_tensor_tensor(x[:], u[:], 1.0, c0_ps[:], ALU.add, ALU.mult)
+        d = f32("d", M)
+        nc.scalar.activation(d[:], v[:], ACT.Copy, scale=-0.25, bias=0.5)
 
         sq = f32("sq", J)
-        for h in range(2):
-            nc.scalar.activation(sq[:, halves[h]], h1[h][:], ACT.Square)
+        nc.scalar.activation(sq[:], h1[:], ACT.Square)
         gq = f32("gq", J)
         nc.scalar.activation(gq[:], sq[:], ACT.Identity, bias=g[:], scale=neg_g[:])
-        gq2 = f32("gq2", J)
-        nc.scalar.activation(gq2[:], gq[:], ACT.Copy, scale=2.0)
-        gq_og = f32("gq_og", J)
+        gq2 = f32("gq2", HALF)
+        nc.scalar.activation(gq2[:], gq[:, halves[0]], ACT.Copy, scale=2.0)
+        gq_og = f32("gq_og", J, tag="v_then_gq_og")
         nc.scalar.activation(gq_og[:], gq[:], ACT.Copy, scale=og_sb[:])
 
-        su = f32("su", M)
-        nc.vector.scalar_tensor_tensor(su[:], s[:], 0.5, u[:], ALU.mult, ALU.mult)
-        nc.vector.tensor_tensor(page_m[:].indirect(idx3[:]), ds_a[:], ds_b[:], ALU.add)
-        hs_a = f32("hs_a", M)
-        nc.vector.scalar_tensor_tensor(hs_a[:], uu[:], -1.0, c0_half[:], ALU.add, ALU.mult)
-        hs_b = f32("hs_b", M)
-        nc.scalar.activation(hs_b[:], su[:], ACT.Copy, bias=-1.0)
+        nc.vector.tensor_tensor(page_m[:].indirect(idx3[:]), x[:], d[:], ALU.mult)
+        w = f32("w", M)
+        nc.vector.tensor_tensor(w[:], u[:], d[:], ALU.mult)
+        e = f32("e", M)
+        nc.scalar.activation(e[:], w[:], ACT.Copy, scale=-1.0, bias=0.5)
 
         da = f32("da", J)
-        nc.vector.tensor_tensor(da[:], page_m[:].indirect(idx2[:]), gq[:], ALU.mult)
-        nc.vector.tensor_tensor(page_j[:].indirect(idx2[:]), da[:], gq2[:], ALU.mult)
-        da_sq = f32("da_sq", J)
-        nc.scalar.activation(da_sq[:], da[:], ACT.Square, scale=2.0)
-        direct = [f32("direct%d" % h, HALF) for h in range(2)]
-        rest = [f32("rest%d" % h, HALF) for h in range(2)]
+        for h in range(2):
+            nc.vector.tensor_tensor(da[:, halves[h]], page_m[:].indirect(idx2[:, list_halves[h]]), gq[:, halves[h]], ALU.mult)
+        hda_sq = f32("hda_sq", J)
+        hda1 = f32("hda1", HALF)
+        nc.scalar.activation(hda_sq[:, halves[0]], da[:, halves[0]], ACT.Square, scale=2.0)
+        nc.scalar.activation(hda1[:], da[:, halves[1]], ACT.Copy, scale=2.0)
+        nc.scalar.activation(hda_sq[:, halves[1]], hda1[:], ACT.Square)
 
-        nc.vector.scalar_tensor_tensor(direct[0][:], da_sq[:, halves[0]], og_sb[:], h1[0][:], ALU.mult, ALU.mult)
-        hds_a = f32("hds_a", M)
-        nc.vector.tensor_tensor(hds_a[:], page_j[:].indirect(idx3[:]), hs_a[:], ALU.mult)
-        nc.vector.scalar_tensor_tensor(direct[1][:], da_sq[:, halves[1]], og_sb[:], h1[1][:], ALU.mult, ALU.mult)
-        nc.vector.tensor_tensor(page_m[:].indirect(idx3[:]), hds_a[:], hs_b[:], ALU.mult)
-        nc.vector.tensor_tensor(rest[0][:], base_sb[:, halves[0]], direct[0][:], ALU.subtract)
+        direct = f32("direct", J)
+        rest = f32("rest", J)
 
-        through = [f32("through%d" % h, HALF) for h in range(2)]
-        res = [f32("res%d" % h, HALF) for h in range(2)]
-        nc.vector.tensor_tensor(through[0][:], page_m[:].indirect(idx2[:, list_halves[0]]), gq_og[:, halves[0]], ALU.mult)
-        nc.vector.tensor_tensor(rest[1][:], base_sb[:, halves[1]], direct[1][:], ALU.subtract)
-        nc.vector.tensor_tensor(res[0][:], through[0][:], rest[0][:], ALU.add)
-        nc.sync.dma_start(out[:, halves[0]], res[0][:])
-        nc.vector.tensor_tensor(through[1][:], page_m[:].indirect(idx2[:, list_halves[1]]), gq_og[:, halves[1]], ALU.mult)
-        nc.vector.tensor_tensor(res[1][:], through[1][:], rest[1][:], ALU.add)
-        nc.scalar.dma_start(out[:, halves[1]], res[1][:])
+        def make_direct(h):
+            nc.vector.scalar_tensor_tensor(direct[:, halves[h]], hda_sq[:, halves[h]], og_sb[:], h1[:, halves[h]], ALU.mult, ALU.mult)
+
+        def make_rest(h):
+            nc.vector.tensor_tensor(rest[:, halves[h]], base_sb[:, halves[h]], direct[:, halves[h]], ALU.subtract)
+
+        nc.vector.tensor_tensor(page_j[:].indirect(idx2[:, list_halves[0]]), da[:, halves[0]], gq2[:], ALU.mult)
+        make_direct(0)
+        nc.vector.tensor_tensor(page_j[:].indirect(idx2[:, list_halves[1]]), hda1[:], gq[:, halves[1]], ALU.mult)
+        make_rest(0)
+        hds_x = f32("hds_x", M)
+        nc.vector.tensor_tensor(hds_x[:], page_j[:].indirect(idx3[:]), x[:], ALU.mult)
+        make_direct(1)
+        nc.vector.tensor_tensor(page_m[:].indirect(idx3[:]), hds_x[:], e[:], ALU.mult)
+        make_rest(1)
+
+        through = f32("through", J)
+        res = f32("res", J)
+        for h in range(2):
+            nc.vector.tensor_tensor(through[:, halves[h]], page_m[:].indirect(idx2[:, list_halves[h]]), gq_og[:, halves[h]], ALU.mult)
+        for h, queue in enumerate((nc.sync, nc.scalar)):
+            nc.vector.tensor_tensor(res[:, halves[h]], through[:, halves[h]], rest[:, halves[h]], ALU.add)
+            queue.dma_start(out[:, halves[h]], res[:, halves[h]])

@@ -21,6 +21,7 @@ PACK = 4
 HALF = J // 2
 COLS = 16
 LEAD = 768
+FIRST = 128
 
 
 def interleaved_views(grouped, raw):
@@ -57,23 +58,23 @@ def tile_attend_gpwriteread_kernel(tc, tab_words, tab_scales, w1, gain, pb, wo, 
         nc.gpsimd.memset(scales[:].bitcast(I32), 0)
         words_hbm = tab_words[0].rearrange("p c t -> p (c t)").bitcast(I32)
         nc.sync.dma_start(idx[:], offs)
-        nc.sync.dma_start(w1_raw[:], w1.rearrange("(p t) r -> p t r", t=PACK))
+        nc.scalar.dma_start(w1_raw[:], w1.rearrange("(p t) r -> p t r", t=PACK))
         nc.sync.dma_start(words[:, :LEAD].bitcast(I32), words_hbm[:, :LEAD])
-        for quad in range(4):
-            nc.sync.dma_start(
-                scales[32 * quad : 32 * quad + 4, :].bitcast(I32),
-                tab_scales[0, 4 * quad : 4 * quad + 4, :].bitcast(I32),
-            )
+        for row in range(4):
+            nc.sync.dma_start(scales[row:P:32, :].bitcast(I32), tab_scales[0, row:16:4, :].bitcast(I32))
         nc.sync.dma_start(words[:, LEAD:].bitcast(I32), words_hbm[:, LEAD:])
         nc.sync.dma_start(g[:], gain)
-        nc.sync.dma_start(idx2[:], offs2)
         nc.sync.dma_start(wo_raw[:], wo.rearrange("(p t) r -> p t r", t=PACK))
+        nc.sync.dma_start(idx2[:], offs2)
         nc.sync.dma_start(dy_raw[:], dy.rearrange("(p t) m -> p t m", t=PACK))
         nc.sync.dma_start(pb_cols[:], pb.rearrange("o (p c) -> p (o c)", c=2))
         nc.sync.dma_start(idx3[:], offs3)
         nc.sync.dma_start(og_sb[:], og)
         nc.sync.dma_start(base_sb[:], base)
 
+        warm = f32("warm", 16)
+        nc.gpsimd.memset(warm[:, 0:1], 0.0)
+        nc.scalar.activation(warm[:, 8:9], warm[:, 0:1], ACT.Silu)
         ident = f32("ident", P)
         make_identity(nc, ident[:])
         page_j = f32("page_j", U)
@@ -90,40 +91,44 @@ def tile_attend_gpwriteread_kernel(tc, tab_words, tab_scales, w1, gain, pb, wo, 
         scales_g = sb.tile([P, J], U8, name="scales_g", align_bytes=64)
         nc.vector.tensor_copy(scales_g[:], scales[:].indirect(idx[:]))
 
-        g_wide = f32("g_wide", HALF)
-        nc.scalar.activation(g_wide[:], g[:, 0:1].to_broadcast([P, HALF]), ACT.Copy)
+        g_wide = f32("g_wide", J - FIRST)
+        nc.scalar.activation(g_wide[:], g[:, 0:1].to_broadcast([P, J - FIRST]), ACT.Copy)
         neg_g = sb.tile([P, 1], F32, name="neg_g")
         nc.scalar.activation(neg_g[:], g[:], ACT.Copy, scale=-1.0)
 
         h1 = f32("h1", J)
+        words_g = [sb.tile([P, HALF], U32, name="words_g%d" % h, tag="stage%d" % h, align_bytes=64) for h in range(2)]
         for h in range(2):
-            words_g = sb.tile([P, HALF], U32, name="words_g%d" % h, tag="stage%d" % h, align_bytes=64)
-            nc.vector.tensor_copy(words_g[:], words[:].indirect(idx[:, list_halves[h]]))
-            a_ps = ps.tile([P, HALF], F32, name="a_ps%d" % h, tag="bank%d" % h)
+            nc.vector.tensor_copy(words_g[h][:], words[:].indirect(idx[:, list_halves[h]]))
+        a_first = ps.tile([P, FIRST], F32, name="a_first")
+        a_rest = ps.tile([P, J - FIRST], F32, name="a_rest", tag="bank1")
+        for dst, lo, hi in ((a_first[:], 0, FIRST), (a_rest[:, : HALF - FIRST], FIRST, HALF), (a_rest[:, HALF - FIRST :], HALF, J)):
             nc.tensor.matmul_mx(
-                out=a_ps[:], lhsT=w1_q[:].bitcast(FP8X4), lhsT_scale=w1_s[:],
-                rhs=words_g[:].bitcast(FP8X4), rhs_scale=scales_g[:, halves[h]], start=True, stop=True,
+                out=dst, lhsT=w1_q[:].bitcast(FP8X4), lhsT_scale=w1_s[:],
+                rhs=words_g[lo // HALF][:, lo % HALF : lo % HALF + hi - lo].bitcast(FP8X4), rhs_scale=scales_g[:, lo:hi],
+                start=True, stop=True,
             )
-            nc.scalar.activation(h1[:, halves[h]], a_ps[:], ACT.Tanh)
+        nc.scalar.activation(h1[:, :FIRST], a_first[:], ACT.Tanh)
+        nc.scalar.activation(h1[:, FIRST:], a_rest[:], ACT.Tanh)
 
-        wo_bf = sb.tile([P, R, PACK], BF16, name="wo_bf", tag="stage0", align_bytes=64)
+        wo_bf = sb.tile([P, R, PACK], BF16, name="wo_bf", align_bytes=64)
         dst, src = interleaved_views(wo_bf, wo_raw)
-        nc.scalar.copy(dst, src)
+        nc.vector.tensor_copy(dst, src)
+        pb_ps = ps.tile([P, 2, P], F32, name="pb_ps", tag="bank1")
+        for c in range(2):
+            nc.tensor.transpose(pb_ps[:, c, :], pb_cols[:, c : c + 1].to_broadcast([P, P]), ident[:])
         dy_bf = sb.tile([P, M, PACK], BF16, name="dy_bf", tag="stage1", align_bytes=64)
         dst, src = interleaved_views(dy_bf, dy_raw)
         nc.scalar.copy(dst, src)
 
-        pb_ps = ps.tile([P, 2, P], F32, name="pb_ps", tag="bank1")
-        for c in range(2):
-            nc.tensor.transpose(pb_ps[:, c, :], pb_cols[:, c : c + 1].to_broadcast([P, P]), ident[:])
         pb_wide = f32("pb_wide", M, tag="dy_then_pb")
         nc.scalar.copy(pb_wide[:].rearrange("p (n c) -> p n c", c=2), pb_ps[:].rearrange("p c n -> p n c"))
 
-        nc.vector.tensor_tensor(page_j[:].indirect(idx2[:, list_halves[0]]), h1[:, halves[0]], g_wide[:], ALU.mult)
+        nc.vector.tensor_tensor(page_j[:].indirect(idx2[:, : FIRST // COLS]), h1[:, :FIRST], g_wide[:, :FIRST], ALU.mult)
         wo_q = sb.tile([P, R], U32, name="wo_q", align_bytes=64)
         wo_s = sb.tile([P, R], U8, name="wo_s", align_bytes=64)
         nc.vector.quantize_mx(out=wo_q[:].bitcast(FP8X4), scales=wo_s[:], in_=wo_bf[:].rearrange("p r t -> p (r t)"))
-        nc.vector.tensor_tensor(page_j[:].indirect(idx2[:, list_halves[1]]), h1[:, halves[1]], g_wide[:], ALU.mult)
+        nc.vector.tensor_tensor(page_j[:].indirect(idx2[:, FIRST // COLS :]), h1[:, FIRST:], g_wide[:], ALU.mult)
         dy_q = sb.tile([P, M], U32, name="dy_q", align_bytes=64)
         dy_s = sb.tile([P, M], U8, name="dy_s", align_bytes=64)
         nc.vector.quantize_mx(out=dy_q[:].bitcast(FP8X4), scales=dy_s[:], in_=dy_bf[:].rearrange("p m t -> p (m t)"))
@@ -137,12 +142,12 @@ def tile_attend_gpwriteread_kernel(tc, tab_words, tab_scales, w1, gain, pb, wo, 
         nc.vector.tensor_tensor(s[:], page_j[:].indirect(idx3[:]), pb_wide[:], ALU.add)
         u = f32("u", M)
         nc.scalar.activation(u[:], s[:], ACT.Tanh, scale=0.5)
-        v = f32("v", M, tag="v_then_gq_og")
-        nc.vector.scalar_tensor_tensor(v[:], u[:], -1.0, s[:], ALU.add, ALU.mult)
+        m = f32("m", M, tag="m_then_gq_og")
+        nc.scalar.activation(m[:], s[:], ACT.Silu, scale=-1.0)
         x = f32("x", M)
         nc.vector.scalar_tensor_tensor(x[:], u[:], 1.0, c0_ps[:], ALU.add, ALU.mult)
         d = f32("d", M)
-        nc.scalar.activation(d[:], v[:], ACT.Copy, scale=-0.25, bias=0.5)
+        nc.vector.tensor_scalar(d[:], m[:], -0.5, 0.5, ALU.mult, ALU.add)
 
         sq = f32("sq", J)
         nc.scalar.activation(sq[:], h1[:], ACT.Square)
@@ -150,7 +155,7 @@ def tile_attend_gpwriteread_kernel(tc, tab_words, tab_scales, w1, gain, pb, wo, 
         nc.scalar.activation(gq[:], sq[:], ACT.Identity, bias=g[:], scale=neg_g[:])
         gq2 = f32("gq2", HALF)
         nc.scalar.activation(gq2[:], gq[:, halves[0]], ACT.Copy, scale=2.0)
-        gq_og = f32("gq_og", J, tag="v_then_gq_og")
+        gq_og = f32("gq_og", J, tag="m_then_gq_og")
         nc.scalar.activation(gq_og[:], gq[:], ACT.Copy, scale=og_sb[:])
 
         nc.vector.tensor_tensor(page_m[:].indirect(idx3[:]), x[:], d[:], ALU.mult)

from contextlib import ExitStack

import concourse.mybir as mybir
from concourse.masks import make_identity

K, R, F, T, J, U, M = 512, 128, 512, 2048, 512, 1024, 256
FLOPS = 2 * K * R * J + 2 * F * R * M

F32 = mybir.dt.float32
BF16 = mybir.dt.bfloat16
I32 = mybir.dt.int32
U32 = mybir.dt.uint32
U16 = mybir.dt.uint16
U8 = mybir.dt.uint8
FP8X4 = mybir.dt.float8_e4m3fn_x4
ACT = mybir.ActivationFunctionType
ALU = mybir.AluOpType

P = 128
PACK = 4
HALF = J // 2
COLS = 16
LEAD = 768
FIRST = 128


def interleaved_views(grouped, raw):
    dst = grouped[:].rearrange("p (c i) t -> p c t i", i=4)
    src = raw[:].rearrange("p t (c i) -> p c t i", i=4)
    return dst, src


def tile_attend_gpwriteread_kernel(tc, tab_words, tab_scales, w1, gain, pb, wo, dy, og, base, offs, offs2, offs3, out):
    nc = tc.nc
    with ExitStack() as ctx:
        sb = ctx.enter_context(tc.tile_pool(name="sb", bufs=1))
        ps = ctx.enter_context(tc.psum_pool(name="ps", bufs=1))

        def f32(name, width, tag=None):
            return sb.tile([P, width], F32, name=name, tag=tag or name, align_bytes=64)

        halves = [slice(h * HALF, (h + 1) * HALF) for h in range(2)]
        list_halves = [slice(h * HALF // COLS, (h + 1) * HALF // COLS) for h in range(2)]

        idx = sb.tile([P, J // COLS], U16, name="idx")
        idx2 = sb.tile([P, J // COLS], U16, name="idx2")
        idx3 = sb.tile([P, M // COLS], U16, name="idx3")
        words = sb.tile([P, T], U32, name="words", align_bytes=64)
        scales = sb.tile([P, T], U8, name="scales", align_bytes=64)
        w1_raw = sb.tile([P, PACK, R], F32, name="w1_raw")
        wo_raw = sb.tile([P, PACK, R], F32, name="wo_raw")
        dy_raw = sb.tile([P, PACK, M], F32, name="dy_raw", tag="dy_then_pb", align_bytes=64)
        base_sb = f32("base_sb", J)
        g = sb.tile([P, 1], F32, name="g")
        og_sb = sb.tile([P, 1], F32, name="og_sb")
        pb_cols = sb.tile([P, 2], F32, name="pb_cols")

        nc.gpsimd.memset(scales[:].bitcast(I32), 0)
        words_hbm = tab_words[0].rearrange("p c t -> p (c t)").bitcast(I32)
        nc.sync.dma_start(idx[:], offs)
        nc.scalar.dma_start(w1_raw[:], w1.rearrange("(p t) r -> p t r", t=PACK))
        nc.sync.dma_start(words[:, :LEAD].bitcast(I32), words_hbm[:, :LEAD])
        for row in range(4):
            nc.sync.dma_start(scales[row:P:32, :].bitcast(I32), tab_scales[0, row:16:4, :].bitcast(I32))
        nc.sync.dma_start(words[:, LEAD:].bitcast(I32), words_hbm[:, LEAD:])
        nc.sync.dma_start(g[:], gain)
        nc.sync.dma_start(wo_raw[:], wo.rearrange("(p t) r -> p t r", t=PACK))
        nc.sync.dma_start(idx2[:], offs2)
        nc.sync.dma_start(dy_raw[:], dy.rearrange("(p t) m -> p t m", t=PACK))
        nc.sync.dma_start(pb_cols[:], pb.rearrange("o (p c) -> p (o c)", c=2))
        nc.sync.dma_start(idx3[:], offs3)
        nc.sync.dma_start(og_sb[:], og)
        nc.sync.dma_start(base_sb[:], base)

        warm = f32("warm", 16)
        nc.gpsimd.memset(warm[:, 0:1], 0.0)
        nc.scalar.activation(warm[:, 8:9], warm[:, 0:1], ACT.Silu)
        ident = f32("ident", P)
        make_identity(nc, ident[:])
        page_j = f32("page_j", U)
        page_m = f32("page_m", U)
        nc.vector.memset(page_j[:], 0.0)
        nc.vector.memset(page_m[:], 0.0)

        w1_bf = sb.tile([P, R, PACK], BF16, name="w1_bf", align_bytes=64)
        dst, src = interleaved_views(w1_bf, w1_raw)
        nc.vector.tensor_copy(dst, src)
        w1_q = sb.tile([P, R], U32, name="w1_q", align_bytes=64)
        w1_s = sb.tile([P, R], U8, name="w1_s", align_bytes=64)
        nc.vector.quantize_mx(out=w1_q[:].bitcast(FP8X4), scales=w1_s[:], in_=w1_bf[:].rearrange("p r t -> p (r t)"))
        scales_g = sb.tile([P, J], U8, name="scales_g", align_bytes=64)
        nc.vector.tensor_copy(scales_g[:], scales[:].indirect(idx[:]))

        g_wide = f32("g_wide", J - FIRST)
        nc.scalar.activation(g_wide[:], g[:, 0:1].to_broadcast([P, J - FIRST]), ACT.Copy)
        neg_g = sb.tile([P, 1], F32, name="neg_g")
        nc.scalar.activation(neg_g[:], g[:], ACT.Copy, scale=-1.0)

        h1 = f32("h1", J)
        words_g = [sb.tile([P, HALF], U32, name="words_g%d" % h, tag="stage%d" % h, align_bytes=64) for h in range(2)]
        for h in range(2):
            nc.vector.tensor_copy(words_g[h][:], words[:].indirect(idx[:, list_halves[h]]))
        a_first = ps.tile([P, FIRST], F32, name="a_first")
        a_rest = ps.tile([P, J - FIRST], F32, name="a_rest", tag="bank1")
        for dst, lo, hi in ((a_first[:], 0, FIRST), (a_rest[:, : HALF - FIRST], FIRST, HALF), (a_rest[:, HALF - FIRST :], HALF, J)):
            nc.tensor.matmul_mx(
                out=dst, lhsT=w1_q[:].bitcast(FP8X4), lhsT_scale=w1_s[:],
                rhs=words_g[lo // HALF][:, lo % HALF : lo % HALF + hi - lo].bitcast(FP8X4), rhs_scale=scales_g[:, lo:hi],
                start=True, stop=True,
            )
        nc.scalar.activation(h1[:, :FIRST], a_first[:], ACT.Tanh)
        nc.scalar.activation(h1[:, FIRST:], a_rest[:], ACT.Tanh)

        wo_bf = sb.tile([P, R, PACK], BF16, name="wo_bf", align_bytes=64)
        dst, src = interleaved_views(wo_bf, wo_raw)
        nc.vector.tensor_copy(dst, src)
        pb_ps = ps.tile([P, 2, P], F32, name="pb_ps", tag="bank1")
        for c in range(2):
            nc.tensor.transpose(pb_ps[:, c, :], pb_cols[:, c : c + 1].to_broadcast([P, P]), ident[:])
        dy_bf = sb.tile([P, M, PACK], BF16, name="dy_bf", tag="stage1", align_bytes=64)
        dst, src = interleaved_views(dy_bf, dy_raw)
        nc.scalar.copy(dst, src)

        pb_wide = f32("pb_wide", M, tag="dy_then_pb")
        nc.scalar.copy(pb_wide[:].rearrange("p (n c) -> p n c", c=2), pb_ps[:].rearrange("p c n -> p n c"))

        nc.vector.tensor_tensor(page_j[:].indirect(idx2[:, : FIRST // COLS]), h1[:, :FIRST], g_wide[:, :FIRST], ALU.mult)
        wo_q = sb.tile([P, R], U32, name="wo_q", align_bytes=64)
        wo_s = sb.tile([P, R], U8, name="wo_s", align_bytes=64)
        nc.vector.quantize_mx(out=wo_q[:].bitcast(FP8X4), scales=wo_s[:], in_=wo_bf[:].rearrange("p r t -> p (r t)"))
        nc.vector.tensor_tensor(page_j[:].indirect(idx2[:, FIRST // COLS :]), h1[:, FIRST:], g_wide[:], ALU.mult)
        dy_q = sb.tile([P, M], U32, name="dy_q", align_bytes=64)
        dy_s = sb.tile([P, M], U8, name="dy_s", align_bytes=64)
        nc.vector.quantize_mx(out=dy_q[:].bitcast(FP8X4), scales=dy_s[:], in_=dy_bf[:].rearrange("p m t -> p (m t)"))
        c0_ps = ps.tile([P, M], F32, name="c0_ps")
        nc.tensor.matmul_mx(
            out=c0_ps[:], lhsT=wo_q[:].bitcast(FP8X4), lhsT_scale=wo_s[:],
            rhs=dy_q[:].bitcast(FP8X4), rhs_scale=dy_s[:], start=True, stop=True,
        )

        s = f32("s", M)
        nc.vector.tensor_tensor(s[:], page_j[:].indirect(idx3[:]), pb_wide[:], ALU.add)
        u = f32("u", M)
        nc.scalar.activation(u[:], s[:], ACT.Tanh, scale=0.5)
        m = f32("m", M, tag="m_then_gq_og")
        nc.scalar.activation(m[:], s[:], ACT.Silu, scale=-1.0)
        x = f32("x", M)
        nc.vector.scalar_tensor_tensor(x[:], u[:], 1.0, c0_ps[:], ALU.add, ALU.mult)
        d = f32("d", M)
        nc.vector.tensor_scalar(d[:], m[:], -0.5, 0.5, ALU.mult, ALU.add)

        sq = f32("sq", J)
        nc.scalar.activation(sq[:], h1[:], ACT.Square)
        gq = f32("gq", J)
        nc.scalar.activation(gq[:], sq[:], ACT.Identity, bias=g[:], scale=neg_g[:])
        gq2 = f32("gq2", HALF)
        nc.scalar.activation(gq2[:], gq[:, halves[0]], ACT.Copy, scale=2.0)
        gq_og = f32("gq_og", J, tag="m_then_gq_og")
        nc.scalar.activation(gq_og[:], gq[:], ACT.Copy, scale=og_sb[:])

        nc.vector.tensor_tensor(page_m[:].indirect(idx3[:]), x[:], d[:], ALU.mult)
        w = f32("w", M)
        nc.vector.tensor_tensor(w[:], u[:], d[:], ALU.mult)
        e = f32("e", M)
        nc.scalar.activation(e[:], w[:], ACT.Copy, scale=-1.0, bias=0.5)

        da = f32("da", J)
        for h in range(2):
            nc.vector.tensor_tensor(da[:, halves[h]], page_m[:].indirect(idx2[:, list_halves[h]]), gq[:, halves[h]], ALU.mult)
        hda_sq = f32("hda_sq", J)
        hda1 = f32("hda1", HALF)
        nc.scalar.activation(hda_sq[:, halves[0]], da[:, halves[0]], ACT.Square, scale=2.0)
        nc.scalar.activation(hda1[:], da[:, halves[1]], ACT.Copy, scale=2.0)
        nc.scalar.activation(hda_sq[:, halves[1]], hda1[:], ACT.Square)

        direct = f32("direct", J)
        rest = f32("rest", J)

        def make_direct(h):
            nc.vector.scalar_tensor_tensor(direct[:, halves[h]], hda_sq[:, halves[h]], og_sb[:], h1[:, halves[h]], ALU.mult, ALU.mult)

        def make_rest(h):
            nc.vector.tensor_tensor(rest[:, halves[h]], base_sb[:, halves[h]], direct[:, halves[h]], ALU.subtract)

        nc.vector.tensor_tensor(page_j[:].indirect(idx2[:, list_halves[0]]), da[:, halves[0]], gq2[:], ALU.mult)
        make_direct(0)
        nc.vector.tensor_tensor(page_j[:].indirect(idx2[:, list_halves[1]]), hda1[:], gq[:, halves[1]], ALU.mult)
        make_rest(0)
        hds_x = f32("hds_x", M)
        nc.vector.tensor_tensor(hds_x[:], page_j[:].indirect(idx3[:]), x[:], ALU.mult)
        make_direct(1)
        nc.vector.tensor_tensor(page_m[:].indirect(idx3[:]), hds_x[:], e[:], ALU.mult)
        make_rest(1)

        through = f32("through", J)
        res = f32("res", J)
        for h in range(2):
            nc.vector.tensor_tensor(through[:, halves[h]], page_m[:].indirect(idx2[:, list_halves[h]]), gq_og[:, halves[h]], ALU.mult)
        for h, queue in enumerate((nc.sync, nc.scalar)):
            nc.vector.tensor_tensor(res[:, halves[h]], through[:, halves[h]], rest[:, halves[h]], ALU.add)
            queue.dma_start(out[:, halves[h]], res[:, halves[h]])
